import numpy as np
import ml_dtypes


def mxq(x, axis, fmt="e4m3"):
    dtype, down = {"e4m3": (ml_dtypes.float8_e4m3fn, 7), "e5m2": (ml_dtypes.float8_e5m2, 14)}[fmt]
    v = np.moveaxis(np.asarray(x, np.float32).astype(ml_dtypes.bfloat16).astype(np.float64), axis, -1)
    blocks = v.reshape(v.shape[:-1] + (-1, 32))
    amax = np.abs(blocks).max(-1, keepdims=True)
    byte = np.maximum(np.where(amax > 0, np.frexp(amax)[1] - 1 + 127, 0) - down, 1)
    scale = np.exp2(byte - 127.0)
    codes = (blocks / scale).astype(np.float32).astype(dtype).astype(np.float64)
    return np.moveaxis((codes * scale).reshape(v.shape), -1, axis)


WIDE = False


def mx_kscale(k):
    if not WIDE:
        return np.ones(k)
    levels = np.array([10, -10, 5, -5, 0])
    if k % 512:
        return np.exp2(np.random.permutation(np.resize(levels, k // 32))).repeat(32)
    a = np.empty((k // 512, 16))
    for p in range(k // 512):
        a[p, :8] = np.random.permutation(np.resize(levels, 8))
        for g in range(8):
            far = levels[np.abs(levels - a[p, g]) >= 10]
            a[p, g + 8] = far[np.random.randint(len(far))]
    return np.exp2(a.ravel()).repeat(32)


def f64(x):
    return np.asarray(x).astype(np.float64)


def striped(idx):
    return np.tile(np.asarray(idx).reshape(-1, 16).T, (8, 1)).astype(np.uint16)


def unstriped(offs):
    return offs[:16].T.reshape(-1).astype(np.int64)


B, N, T, D, DV, NQ = 1, 512, 2048, 512, 256, 128


def setup_inputs():
    n = np.random.standard_normal
    idx = np.random.permutation(T)[:B * N]
    s = mx_kscale(D)[:, None]
    u = np.ones(T)
    u[idx] = mx_kscale(B * N)
    r = np.random.uniform(0.5, 2.0, T)
    long = np.random.uniform(0.9, 1.1, T)
    k = n((D, T)) / s * long
    v = n((DV, T)) / (u * r)
    return {
        "qT": (n((B, D, NQ)) * s * (0.80 / np.sqrt(D))).astype(np.float32),
        "kT": k.astype(np.float32),
        "vT": v.astype(np.float32),
        "vs": np.tile(u * r, (128, 1)).astype(np.float32),
        "kb": np.tile(-0.5 * np.sum(np.square(k * s), 0) * (0.80 / np.sqrt(D)), (128, 1)).astype(np.float32),
        "og": n((B, NQ, DV)).astype(np.float32),
        "offs": striped(idx),
    }


def reference(qT, kT, vT, vs, kb, og, offs):
    idx = unstriped(offs)
    k = f64(kT)
    v = f64(vT)
    pick = lambda x: x[:, idx].reshape(x.shape[0], B, N).transpose(1, 0, 2)
    q = f64(qT)
    score = mxq(q, 1, "e4m3").transpose(0, 2, 1) @ mxq(pick(k), 1, "e4m3")
    score = score + pick(f64(kb))[:, :1, :]
    m = score.max(-1, keepdims=True)
    p = np.exp(score - m)
    total = p.sum(-1, keepdims=True)
    w = p * pick(f64(vs))[:, :1, :]
    y = mxq(w, 2, "e4m3") @ mxq(pick(v).transpose(0, 2, 1), 1, "e4m3")
    y = y / total
    y = y / (1.0 + np.exp(-f64(og)))
    return y

@@ -1,0 +1,188 @@
+from contextlib import ExitStack
+
+import concourse.mybir as mybir
+from concourse.masks import make_identity
+
+F32 = mybir.dt.float32
+BF16 = mybir.dt.bfloat16
+U32 = mybir.dt.uint32
+U16 = mybir.dt.uint16
+U8 = mybir.dt.uint8
+FP8X4 = mybir.dt.float8_e4m3fn_x4
+ADD = mybir.AluOpType.add
+SUB = mybir.AluOpType.subtract
+MULT = mybir.AluOpType.mult
+MIN = mybir.AluOpType.min
+ACT = mybir.ActivationFunctionType
+AXIS_X = mybir.AxisListType.X
+
+P = 128
+PACK = 4
+N = 512
+T = 2048
+D = 512
+DV = 256
+NQ = 128
+
+FLOPS = 2 * NQ * N * D + 2 * NQ * N * DV
+BYTES = 4 * (D * NQ + D * T + DV * T + 2 * T + 2 * NQ * DV) + 2 * P * (N // 16)
+
+
+def tile_attend_x_norm_gate_topk_kernel(tc, qT, kT, vT, vs, kb, og, offs, out):
+    nc = tc.nc
+    with ExitStack() as ctx:
+        keep = ctx.enter_context(tc.tile_pool(name="keep", bufs=1))
+        psum = ctx.enter_context(tc.psum_pool(name="psum", bufs=1))
+
+        offsets = keep.tile([P, N // 16], U16, name="offsets")
+        q_raw = keep.tile([P, PACK, NQ], F32, name="q_raw")
+        k_pool = [keep.tile([P, T], F32, name="k_pool%d" % t) for t in range(PACK)]
+        v_pool = [keep.tile([P, T], F32, name="v_pool%d" % b) for b in range(2)]
+        kb_pool = keep.tile([P, T], F32, name="kb_pool")
+        vs_pool = keep.tile([P, T], F32, name="vs_pool")
+        gate_raw = keep.tile([P, DV], F32, name="gate_raw")
+        warm = keep.tile([P, 1], F32, name="warm")
+        ident = keep.tile([P, P], F32, name="ident")
+
+        nc.vector.memset(warm[:], 0.0)
+        nc.vector.memset(kb_pool[:], 0.0)
+        nc.vector.memset(vs_pool[:], 0.0)
+        nc.sync.dma_start(offsets[:], offs)
+        nc.sync.dma_start(out=q_raw[:], in_=qT.rearrange("b (p t) q -> p (b t) q", t=PACK))
+        k_rows = kT.rearrange("(p t) n -> p t n", t=PACK)
+        for t in range(PACK):
+            nc.sync.dma_start(out=k_pool[t][:], in_=k_rows[:, t, :])
+            if t == 0:
+                nc.sync.dma_start(out=kb_pool[0:1, :], in_=kb[0:1, :])
+                nc.sync.dma_start(out=vs_pool[0:1, :], in_=vs[0:1, :])
+        for b in range(2):
+            nc.sync.dma_start(out=v_pool[b][:], in_=vT[b * P : (b + 1) * P, :])
+        nc.sync.dma_start(out=gate_raw[:], in_=og.rearrange("b q e -> (b q) e"))
+
+        make_identity(nc, ident[:])
+        warm_out = keep.tile([P, 1], F32, name="warm_out")
+        nc.scalar.activation(warm_out[:], warm[:], ACT.Exp)
+
+        q_grouped = keep.tile([P, NQ, PACK], BF16, name="q_grouped", align_bytes=64)
+        q_codes = keep.tile([P, NQ], U32, name="q_codes", align_bytes=64)
+        q_scales = keep.tile([P, NQ], U8, name="q_scales", align_bytes=64)
+        nc.scalar.copy(q_grouped[:], q_raw[:].rearrange("p t q -> p q t"))
+        nc.vector.quantize_mx(
+            out=q_codes[:].bitcast(FP8X4), scales=q_scales[:], in_=q_grouped[:].rearrange("p q t -> p (q t)")
+        )
+
+        kb_row = keep.tile([P, N], F32, name="kb_row")
+        nc.vector.tensor_copy(kb_row[:], kb_pool[:].indirect(offsets[:]))
+        kb_turned = psum.tile([P, 4, P], F32, name="kb_turned", tag="bank_a")
+        for c in range(4):
+            nc.tensor.transpose(kb_turned[:, c, :], kb_row[:, c * P : (c + 1) * P], ident[:])
+        kb_cols = keep.tile([P, 4], F32, name="kb_cols")
+        nc.scalar.copy(kb_cols[:], kb_turned[:, :, 0])
+        kb_spread = psum.tile([P, 4, P], F32, name="kb_spread", tag="bank_b")
+        for c in range(4):
+            nc.tensor.transpose(kb_spread[:, c, :], kb_cols[:, c : c + 1].to_broadcast([P, P]), ident[:])
+        neg_kb = keep.tile([P, N], F32, name="neg_kb")
+        nc.scalar.activation(neg_kb[:], kb_spread[:].rearrange("p c q -> p (c q)"), ACT.Copy, scale=-1.0)
+
+        vs_row = keep.tile([P, N], F32, name="vs_row")
+        nc.vector.tensor_copy(vs_row[:], vs_pool[:].indirect(offsets[:]))
+        vs_turned = psum.tile([P, PACK, P], F32, name="vs_turned", tag="bank_a")
+        for t in range(PACK):
+            nc.tensor.transpose(vs_turned[:, t, :], vs_row[:, t:N:PACK], ident[:])
+        vs_cols = keep.tile([P, PACK], F32, name="vs_cols")
+        nc.scalar.copy(vs_cols[:], vs_turned[:, :, 0])
+
+        k_grouped = keep.tile([P, N, PACK], BF16, name="k_grouped", align_bytes=64)
+        for t in range(PACK):
+            nc.vector.tensor_copy(k_grouped[:, :, t], k_pool[t][:].indirect(offsets[:]))
+        k_codes = keep.tile([P, N], U32, name="k_codes", align_bytes=64)
+        k_scales = keep.tile([P, N], U8, name="k_scales", align_bytes=64)
+        k_flat = k_grouped[:].rearrange("p n t -> p (n t)")
+        half = N // 2
+        for h in range(2):
+            nc.vector.quantize_mx(
+                out=k_codes[:, h * half : (h + 1) * half].bitcast(FP8X4),
+                scales=k_scales[:, h * half : (h + 1) * half],
+                in_=k_flat[:, h * half * PACK : (h + 1) * half * PACK],
+            )
+        scores = [psum.tile([P, half], F32, name="scores%d" % h, tag="bank_s%d" % h) for h in range(2)]
+        neg_s = keep.tile([P, N], F32, name="neg_s")
+        for h in range(2):
+            cols = slice(h * half, (h + 1) * half)
+            nc.tensor.matmul_mx(
+                out=scores[h][:],
+                lhsT=q_codes[:].bitcast(FP8X4),
+                lhsT_scale=q_scales[:],
+                rhs=k_codes[:, cols].bitcast(FP8X4),
+                rhs_scale=k_scales[:, cols],
+                start=True,
+                stop=True,
+            )
+        for h in range(2):
+            cols = slice(h * half, (h + 1) * half)
+            nc.vector.tensor_tensor(neg_s[:, cols], neg_kb[:, cols], scores[h][:], SUB)
+        neg_m = keep.tile([P, 1], F32, name="neg_m")
+        nc.vector.tensor_reduce(neg_m[:], neg_s[:], AXIS_X, MIN)
+
+        p = keep.tile([P, PACK, P], F32, name="p")
+        total = keep.tile([P, 1], F32, name="total")
+        nc.scalar.activation(
+            p[:].rearrange("q t s -> q s t"),
+            neg_s[:].rearrange("q (s t) -> q s t", t=PACK),
+            ACT.Exp,
+            bias=neg_m[:],
+            scale=-1.0,
+            accum_out=total[:],
+        )
+        p_turned = psum.tile([P, PACK, NQ], F32, name="p_turned", tag="bank_p")
+        for t in range(PACK):
+            nc.tensor.transpose(p_turned[:, t, :], p[:, t, :], ident[:])
+        w = keep.tile([P, NQ, PACK], BF16, name="w", align_bytes=64)
+        w_codes = keep.tile([P, NQ], U32, name="w_codes", align_bytes=64)
+        w_scales = keep.tile([P, NQ], U8, name="w_scales", align_bytes=64)
+        nc.vector.tensor_tensor(
+            w[:],
+            p_turned[:].rearrange("s t q -> s q t"),
+            vs_cols[:].unsqueeze(1).to_broadcast([P, NQ, PACK]),
+            MULT,
+        )
+        nc.vector.quantize_mx(
+            out=w_codes[:].bitcast(FP8X4), scales=w_scales[:], in_=w[:].rearrange("p q t -> p (q t)")
+        )
+        inv_total = keep.tile([P, 1], F32, name="inv_total")
+        nc.vector.reciprocal(inv_total[:], total[:])
+
+        gate_tanh = keep.tile([P, DV], F32, name="gate_tanh")
+        gate = keep.tile([P, DV], F32, name="gate")
+        nc.scalar.activation(gate_tanh[:], gate_raw[:], ACT.Tanh, scale=0.5)
+        nc.scalar.activation(gate[:], gate_tanh[:], ACT.Copy, scale=0.5, bias=0.5)
+
+        result = keep.tile([P, DV], F32, name="result")
+        out_rows = out.rearrange("b q e -> (b q) e")
+        for b in range(2):
+            v_words = keep.tile([P, 2, P, 2], BF16, name="v_words%d" % b)
+            nc.vector.tensor_copy(v_words[:].rearrange("e u s r -> e s u r"), v_pool[b][:].indirect(offsets[:]))
+            words = v_words[:].rearrange("e u s r -> e (u s r)").bitcast(F32)
+            v_turned = psum.tile([P, 2, P], F32, name="v_turned%d" % b, tag="bank_v%d" % b)
+            for u in range(2):
+                nc.tensor.transpose(v_turned[:, u, :], words[:, u * P : (u + 1) * P], ident[:])
+            v_grouped = keep.tile([P, P * PACK], BF16, name="v_grouped%d" % b, align_bytes=64)
+            nc.scalar.copy(
+                v_grouped[:].bitcast(F32).rearrange("s (e u) -> s e u", u=2), v_turned[:].rearrange("s u e -> s e u")
+            )
+            v_codes = keep.tile([P, P], U32, name="v_codes%d" % b, align_bytes=64)
+            v_scales = keep.tile([P, P], U8, name="v_scales%d" % b, align_bytes=64)
+            nc.vector.quantize_mx(out=v_codes[:].bitcast(FP8X4), scales=v_scales[:], in_=v_grouped[:])
+            y = psum.tile([P, P], F32, name="y%d" % b, tag="bank_%s" % "ab"[b])
+            nc.tensor.matmul_mx(
+                out=y[:],
+                lhsT=w_codes[:].bitcast(FP8X4),
+                lhsT_scale=w_scales[:],
+                rhs=v_codes[:].bitcast(FP8X4),
+                rhs_scale=v_scales[:],
+                start=True,
+                stop=True,
+            )
+            cols = slice(b * P, (b + 1) * P)
+            nc.vector.scalar_tensor_tensor(result[:, cols], y[:], inv_total[:], gate[:, cols], MULT, MULT)
+            nc.sync.dma_start(out=out_rows[:, cols], in_=result[:, cols])

@@ -48,29 +48,29 @@ def tile_attend_x_norm_gate_topk_kernel(tc, qT, kT, vT, vs, kb, og, offs, out):
         nc.vector.memset(kb_pool[:], 0.0)
         nc.vector.memset(vs_pool[:], 0.0)
         nc.sync.dma_start(offsets[:], offs)
-        nc.sync.dma_start(out=q_raw[:], in_=qT.rearrange("b (p t) q -> p (b t) q", t=PACK))
         k_rows = kT.rearrange("(p t) n -> p t n", t=PACK)
         for t in range(PACK):
             nc.sync.dma_start(out=k_pool[t][:], in_=k_rows[:, t, :])
             if t == 0:
                 nc.sync.dma_start(out=kb_pool[0:1, :], in_=kb[0:1, :])
+            if t == 1:
                 nc.sync.dma_start(out=vs_pool[0:1, :], in_=vs[0:1, :])
+        nc.sync.dma_start(out=q_raw[:], in_=qT.rearrange("b (p t) q -> p (b t) q", t=PACK))
         for b in range(2):
             nc.sync.dma_start(out=v_pool[b][:], in_=vT[b * P : (b + 1) * P, :])
         nc.sync.dma_start(out=gate_raw[:], in_=og.rearrange("b q e -> (b q) e"))
-
         make_identity(nc, ident[:])
         warm_out = keep.tile([P, 1], F32, name="warm_out")
         nc.scalar.activation(warm_out[:], warm[:], ACT.Exp)
 
-        q_grouped = keep.tile([P, NQ, PACK], BF16, name="q_grouped", align_bytes=64)
-        q_codes = keep.tile([P, NQ], U32, name="q_codes", align_bytes=64)
-        q_scales = keep.tile([P, NQ], U8, name="q_scales", align_bytes=64)
-        nc.scalar.copy(q_grouped[:], q_raw[:].rearrange("p t q -> p q t"))
-        nc.vector.quantize_mx(
-            out=q_codes[:].bitcast(FP8X4), scales=q_scales[:], in_=q_grouped[:].rearrange("p q t -> p (q t)")
-        )
+        k_grouped = keep.tile([P, N, PACK], BF16, name="k_grouped", align_bytes=64)
+        idle_bank = psum.tile([P, 4, P], F32, name="idle_bank", tag="bank_idle")
 
+        def keep_clock(pool, count):
+            for c in range(count):
+                nc.tensor.transpose(idle_bank[:, c % 4, :], pool[:, c * P : (c + 1) * P], ident[:])
+
+        nc.vector.tensor_copy(k_grouped[:, :, 0], k_pool[0][:].indirect(offsets[:]))
         kb_row = keep.tile([P, N], F32, name="kb_row")
         nc.vector.tensor_copy(kb_row[:], kb_pool[:].indirect(offsets[:]))
         kb_turned = psum.tile([P, 4, P], F32, name="kb_turned", tag="bank_a")
@@ -84,6 +84,7 @@ def tile_attend_x_norm_gate_topk_kernel(tc, qT, kT, vT, vs, kb, og, offs, out):
         neg_kb = keep.tile([P, N], F32, name="neg_kb")
         nc.scalar.activation(neg_kb[:], kb_spread[:].rearrange("p c q -> p (c q)"), ACT.Copy, scale=-1.0)
 
+        nc.vector.tensor_copy(k_grouped[:, :, 1], k_pool[1][:].indirect(offsets[:]))
         vs_row = keep.tile([P, N], F32, name="vs_row")
         nc.vector.tensor_copy(vs_row[:], vs_pool[:].indirect(offsets[:]))
         vs_turned = psum.tile([P, PACK, P], F32, name="vs_turned", tag="bank_a")
@@ -92,9 +93,18 @@ def tile_attend_x_norm_gate_topk_kernel(tc, qT, kT, vT, vs, kb, og, offs, out):
         vs_cols = keep.tile([P, PACK], F32, name="vs_cols")
         nc.scalar.copy(vs_cols[:], vs_turned[:, :, 0])
 
-        k_grouped = keep.tile([P, N, PACK], BF16, name="k_grouped", align_bytes=64)
-        for t in range(PACK):
-            nc.vector.tensor_copy(k_grouped[:, :, t], k_pool[t][:].indirect(offsets[:]))
+        nc.vector.tensor_copy(k_grouped[:, :, 2], k_pool[2][:].indirect(offsets[:]))
+        nc.vector.tensor_copy(k_grouped[:, :, 3], k_pool[3][:].indirect(offsets[:]))
+        q_grouped = keep.tile([P, NQ, PACK], BF16, name="q_grouped", align_bytes=64)
+        q_codes = keep.tile([P, NQ], U32, name="q_codes", align_bytes=64)
+        q_scales = keep.tile([P, NQ], U8, name="q_scales", align_bytes=64)
+        nc.scalar.copy(q_grouped[:], q_raw[:].rearrange("p t q -> p q t"))
+        nc.vector.quantize_mx(
+            out=q_codes[:].bitcast(FP8X4), scales=q_scales[:], in_=q_grouped[:].rearrange("p q t -> p (q t)")
+        )
+
+        keep_clock(k_pool[2], 14)
+        keep_clock(k_pool[3], 14)
         k_codes = keep.tile([P, N], U32, name="k_codes", align_bytes=64)
         k_scales = keep.tile([P, N], U8, name="k_scales", align_bytes=64)
         k_flat = k_grouped[:].rearrange("p n t -> p (n t)")
@@ -118,6 +128,44 @@ def tile_attend_x_norm_gate_topk_kernel(tc, qT, kT, vT, vs, kb, og, offs, out):
                 start=True,
                 stop=True,
             )
+        v_words = []
+        v_grouped = []
+        v_codes = keep.tile([P, DV], U32, name="v_codes", align_bytes=64)
+        v_scales = keep.tile([P, DV], U8, name="v_scales", align_bytes=64)
+
+        v_cast = keep.tile([P, T], BF16, name="v_cast")
+
+        def gather_values(b):
+            words = keep.tile([P, 2, P, 2], BF16, name="v_words%d" % b)
+            columns = words[:].rearrange("e u s r -> e s u r")
+            if b == 0:
+                nc.scalar.activation(columns, v_cast[:].indirect(offsets[:]), ACT.Copy)
+            else:
+                nc.vector.tensor_copy(columns, v_pool[b][:].indirect(offsets[:]))
+            v_words.append(words)
+
+        def turn_values(b):
+            words = v_words[b][:].rearrange("e u s r -> e (u s r)").bitcast(F32)
+            turned = psum.tile([P, 2, P], F32, name="v_turned%d" % b, tag="bank_v%d" % b)
+            for u in range(2):
+                nc.tensor.transpose(turned[:, u, :], words[:, u * P : (u + 1) * P], ident[:])
+            grouped = keep.tile([P, P * PACK], BF16, name="v_grouped%d" % b, align_bytes=64)
+            nc.scalar.copy(
+                grouped[:].bitcast(F32).rearrange("s (e u) -> s e u", u=2), turned[:].rearrange("s u e -> s e u")
+            )
+            v_grouped.append(grouped)
+
+        def quantize_values(b):
+            cols = slice(b * P, (b + 1) * P)
+            nc.vector.quantize_mx(
+                out=v_codes[:, cols].bitcast(FP8X4), scales=v_scales[:, cols], in_=v_grouped[b][:]
+            )
+
+        keep_clock(v_pool[0], 10)
+        nc.vector.tensor_copy(v_cast[:, T // 2 :], v_pool[0][:, T // 2 :])
+        nc.scalar.activation(v_cast[:, : T // 2], v_pool[0][:, : T // 2], ACT.Copy)
+        gather_values(0)
+        keep_clock(v_pool[1], 8)
         for h in range(2):
             cols = slice(h * half, (h + 1) * half)
             nc.vector.tensor_tensor(neg_s[:, cols], neg_kb[:, cols], scores[h][:], SUB)
@@ -137,6 +185,9 @@ def tile_attend_x_norm_gate_topk_kernel(tc, qT, kT, vT, vs, kb, og, offs, out):
         p_turned = psum.tile([P, PACK, NQ], F32, name="p_turned", tag="bank_p")
         for t in range(PACK):
             nc.tensor.transpose(p_turned[:, t, :], p[:, t, :], ident[:])
+        turn_values(0)
+        gather_values(1)
+        quantize_values(0)
         w = keep.tile([P, NQ, PACK], BF16, name="w", align_bytes=64)
         w_codes = keep.tile([P, NQ], U32, name="w_codes", align_bytes=64)
         w_scales = keep.tile([P, NQ], U8, name="w_scales", align_bytes=64)
@@ -146,43 +197,36 @@ def tile_attend_x_norm_gate_topk_kernel(tc, qT, kT, vT, vs, kb, og, offs, out):
             vs_cols[:].unsqueeze(1).to_broadcast([P, NQ, PACK]),
             MULT,
         )
+        turn_values(1)
         nc.vector.quantize_mx(
             out=w_codes[:].bitcast(FP8X4), scales=w_scales[:], in_=w[:].rearrange("p q t -> p (q t)")
         )
+        quantize_values(1)
         inv_total = keep.tile([P, 1], F32, name="inv_total")
         nc.vector.reciprocal(inv_total[:], total[:])
 
         gate_tanh = keep.tile([P, DV], F32, name="gate_tanh")
         gate = keep.tile([P, DV], F32, name="gate")
         nc.scalar.activation(gate_tanh[:], gate_raw[:], ACT.Tanh, scale=0.5)
-        nc.scalar.activation(gate[:], gate_tanh[:], ACT.Copy, scale=0.5, bias=0.5)
+        nc.vector.tensor_scalar(gate[:], gate_tanh[:], 1.0, inv_total[:], ADD, MULT)
 
         result = keep.tile([P, DV], F32, name="result")
         out_rows = out.rearrange("b q e -> (b q) e")
+        y = []
         for b in range(2):
-            v_words = keep.tile([P, 2, P, 2], BF16, name="v_words%d" % b)
-            nc.vector.tensor_copy(v_words[:].rearrange("e u s r -> e s u r"), v_pool[b][:].indirect(offsets[:]))
-            words = v_words[:].rearrange("e u s r -> e (u s r)").bitcast(F32)
-            v_turned = psum.tile([P, 2, P], F32, name="v_turned%d" % b, tag="bank_v%d" % b)
-            for u in range(2):
-                nc.tensor.transpose(v_turned[:, u, :], words[:, u * P : (u + 1) * P], ident[:])
-            v_grouped = keep.tile([P, P * PACK], BF16, name="v_grouped%d" % b, align_bytes=64)
-            nc.scalar.copy(
-                v_grouped[:].bitcast(F32).rearrange("s (e u) -> s e u", u=2), v_turned[:].rearrange("s u e -> s e u")
-            )
-            v_codes = keep.tile([P, P], U32, name="v_codes%d" % b, align_bytes=64)
-            v_scales = keep.tile([P, P], U8, name="v_scales%d" % b, align_bytes=64)
-            nc.vector.quantize_mx(out=v_codes[:].bitcast(FP8X4), scales=v_scales[:], in_=v_grouped[:])
-            y = psum.tile([P, P], F32, name="y%d" % b, tag="bank_%s" % "ab"[b])
+            cols = slice(b * P, (b + 1) * P)
+            acc = psum.tile([P, P], F32, name="y%d" % b, tag="bank_%s" % "ab"[b])
             nc.tensor.matmul_mx(
-                out=y[:],
+                out=acc[:],
                 lhsT=w_codes[:].bitcast(FP8X4),
                 lhsT_scale=w_scales[:],
-                rhs=v_codes[:].bitcast(FP8X4),
-                rhs_scale=v_scales[:],
+                rhs=v_codes[:, cols].bitcast(FP8X4),
+                rhs_scale=v_scales[:, cols],
                 start=True,
                 stop=True,
             )
+            y.append(acc)
+        for b in range(2):
             cols = slice(b * P, (b + 1) * P)
-            nc.vector.scalar_tensor_tensor(result[:, cols], y[:], inv_total[:], gate[:, cols], MULT, MULT)
+            nc.vector.scalar_tensor_tensor(result[:, cols], y[b][:], 0.5, gate[:, cols], MULT, MULT)
             nc.sync.dma_start(out=out_rows[:, cols], in_=result[:, cols])

from contextlib import ExitStack

import concourse.mybir as mybir
from concourse.masks import make_identity

F32 = mybir.dt.float32
BF16 = mybir.dt.bfloat16
U32 = mybir.dt.uint32
U16 = mybir.dt.uint16
U8 = mybir.dt.uint8
FP8X4 = mybir.dt.float8_e4m3fn_x4
ADD = mybir.AluOpType.add
SUB = mybir.AluOpType.subtract
MULT = mybir.AluOpType.mult
MIN = mybir.AluOpType.min
ACT = mybir.ActivationFunctionType
AXIS_X = mybir.AxisListType.X

P = 128
PACK = 4
N = 512
T = 2048
D = 512
DV = 256
NQ = 128

FLOPS = 2 * NQ * N * D + 2 * NQ * N * DV
BYTES = 4 * (D * NQ + D * T + DV * T + 2 * T + 2 * NQ * DV) + 2 * P * (N // 16)


def tile_attend_x_norm_gate_topk_kernel(tc, qT, kT, vT, vs, kb, og, offs, out):
    nc = tc.nc
    with ExitStack() as ctx:
        keep = ctx.enter_context(tc.tile_pool(name="keep", bufs=1))
        psum = ctx.enter_context(tc.psum_pool(name="psum", bufs=1))

        offsets = keep.tile([P, N // 16], U16, name="offsets")
        q_raw = keep.tile([P, PACK, NQ], F32, name="q_raw")
        k_pool = [keep.tile([P, T], F32, name="k_pool%d" % t) for t in range(PACK)]
        v_pool = [keep.tile([P, T], F32, name="v_pool%d" % b) for b in range(2)]
        kb_pool = keep.tile([P, T], F32, name="kb_pool")
        vs_pool = keep.tile([P, T], F32, name="vs_pool")
        gate_raw = keep.tile([P, DV], F32, name="gate_raw")
        warm = keep.tile([P, 1], F32, name="warm")
        ident = keep.tile([P, P], F32, name="ident")

        nc.vector.memset(warm[:], 0.0)
        nc.vector.memset(kb_pool[:], 0.0)
        nc.vector.memset(vs_pool[:], 0.0)
        nc.sync.dma_start(offsets[:], offs)
        k_rows = kT.rearrange("(p t) n -> p t n", t=PACK)
        for t in range(PACK):
            nc.sync.dma_start(out=k_pool[t][:], in_=k_rows[:, t, :])
            if t == 0:
                nc.sync.dma_start(out=kb_pool[0:1, :], in_=kb[0:1, :])
            if t == 1:
                nc.sync.dma_start(out=vs_pool[0:1, :], in_=vs[0:1, :])
        nc.sync.dma_start(out=q_raw[:], in_=qT.rearrange("b (p t) q -> p (b t) q", t=PACK))
        for b in range(2):
            nc.sync.dma_start(out=v_pool[b][:], in_=vT[b * P : (b + 1) * P, :])
        nc.sync.dma_start(out=gate_raw[:], in_=og.rearrange("b q e -> (b q) e"))
        make_identity(nc, ident[:])
        warm_out = keep.tile([P, 1], F32, name="warm_out")
        nc.scalar.activation(warm_out[:], warm[:], ACT.Exp)

        k_grouped = keep.tile([P, N, PACK], BF16, name="k_grouped", align_bytes=64)
        idle_bank = psum.tile([P, 4, P], F32, name="idle_bank", tag="bank_idle")

        def keep_clock(pool, count):
            for c in range(count):
                nc.tensor.transpose(idle_bank[:, c % 4, :], pool[:, c * P : (c + 1) * P], ident[:])

        nc.vector.tensor_copy(k_grouped[:, :, 0], k_pool[0][:].indirect(offsets[:]))
        kb_row = keep.tile([P, N], F32, name="kb_row")
        nc.vector.tensor_copy(kb_row[:], kb_pool[:].indirect(offsets[:]))
        kb_turned = psum.tile([P, 4, P], F32, name="kb_turned", tag="bank_a")
        for c in range(4):
            nc.tensor.transpose(kb_turned[:, c, :], kb_row[:, c * P : (c + 1) * P], ident[:])
        kb_cols = keep.tile([P, 4], F32, name="kb_cols")
        nc.scalar.copy(kb_cols[:], kb_turned[:, :, 0])
        kb_spread = psum.tile([P, 4, P], F32, name="kb_spread", tag="bank_b")
        for c in range(4):
            nc.tensor.transpose(kb_spread[:, c, :], kb_cols[:, c : c + 1].to_broadcast([P, P]), ident[:])
        neg_kb = keep.tile([P, N], F32, name="neg_kb")
        nc.scalar.activation(neg_kb[:], kb_spread[:].rearrange("p c q -> p (c q)"), ACT.Copy, scale=-1.0)

        nc.vector.tensor_copy(k_grouped[:, :, 1], k_pool[1][:].indirect(offsets[:]))
        vs_row = keep.tile([P, N], F32, name="vs_row")
        nc.vector.tensor_copy(vs_row[:], vs_pool[:].indirect(offsets[:]))
        vs_turned = psum.tile([P, PACK, P], F32, name="vs_turned", tag="bank_a")
        for t in range(PACK):
            nc.tensor.transpose(vs_turned[:, t, :], vs_row[:, t:N:PACK], ident[:])
        vs_cols = keep.tile([P, PACK], F32, name="vs_cols")
        nc.scalar.copy(vs_cols[:], vs_turned[:, :, 0])

        nc.vector.tensor_copy(k_grouped[:, :, 2], k_pool[2][:].indirect(offsets[:]))
        nc.vector.tensor_copy(k_grouped[:, :, 3], k_pool[3][:].indirect(offsets[:]))
        q_grouped = keep.tile([P, NQ, PACK], BF16, name="q_grouped", align_bytes=64)
        q_codes = keep.tile([P, NQ], U32, name="q_codes", align_bytes=64)
        q_scales = keep.tile([P, NQ], U8, name="q_scales", align_bytes=64)
        nc.scalar.copy(q_grouped[:], q_raw[:].rearrange("p t q -> p q t"))
        nc.vector.quantize_mx(
            out=q_codes[:].bitcast(FP8X4), scales=q_scales[:], in_=q_grouped[:].rearrange("p q t -> p (q t)")
        )

        keep_clock(k_pool[2], 14)
        keep_clock(k_pool[3], 14)
        k_codes = keep.tile([P, N], U32, name="k_codes", align_bytes=64)
        k_scales = keep.tile([P, N], U8, name="k_scales", align_bytes=64)
        k_flat = k_grouped[:].rearrange("p n t -> p (n t)")
        half = N // 2
        for h in range(2):
            nc.vector.quantize_mx(
                out=k_codes[:, h * half : (h + 1) * half].bitcast(FP8X4),
                scales=k_scales[:, h * half : (h + 1) * half],
                in_=k_flat[:, h * half * PACK : (h + 1) * half * PACK],
            )
        scores = [psum.tile([P, half], F32, name="scores%d" % h, tag="bank_s%d" % h) for h in range(2)]
        neg_s = keep.tile([P, N], F32, name="neg_s")
        for h in range(2):
            cols = slice(h * half, (h + 1) * half)
            nc.tensor.matmul_mx(
                out=scores[h][:],
                lhsT=q_codes[:].bitcast(FP8X4),
                lhsT_scale=q_scales[:],
                rhs=k_codes[:, cols].bitcast(FP8X4),
                rhs_scale=k_scales[:, cols],
                start=True,
                stop=True,
            )
        v_words = []
        v_grouped = []
        v_codes = keep.tile([P, DV], U32, name="v_codes", align_bytes=64)
        v_scales = keep.tile([P, DV], U8, name="v_scales", align_bytes=64)

        v_cast = keep.tile([P, T], BF16, name="v_cast")

        def gather_values(b):
            words = keep.tile([P, 2, P, 2], BF16, name="v_words%d" % b)
            columns = words[:].rearrange("e u s r -> e s u r")
            if b == 0:
                nc.scalar.activation(columns, v_cast[:].indirect(offsets[:]), ACT.Copy)
            else:
                nc.vector.tensor_copy(columns, v_pool[b][:].indirect(offsets[:]))
            v_words.append(words)

        def turn_values(b):
            words = v_words[b][:].rearrange("e u s r -> e (u s r)").bitcast(F32)
            turned = psum.tile([P, 2, P], F32, name="v_turned%d" % b, tag="bank_v%d" % b)
            for u in range(2):
                nc.tensor.transpose(turned[:, u, :], words[:, u * P : (u + 1) * P], ident[:])
            grouped = keep.tile([P, P * PACK], BF16, name="v_grouped%d" % b, align_bytes=64)
            nc.scalar.copy(
                grouped[:].bitcast(F32).rearrange("s (e u) -> s e u", u=2), turned[:].rearrange("s u e -> s e u")
            )
            v_grouped.append(grouped)

        def quantize_values(b):
            cols = slice(b * P, (b + 1) * P)
            nc.vector.quantize_mx(
                out=v_codes[:, cols].bitcast(FP8X4), scales=v_scales[:, cols], in_=v_grouped[b][:]
            )

        keep_clock(v_pool[0], 10)
        nc.vector.tensor_copy(v_cast[:, T // 2 :], v_pool[0][:, T // 2 :])
        nc.scalar.activation(v_cast[:, : T // 2], v_pool[0][:, : T // 2], ACT.Copy)
        gather_values(0)
        keep_clock(v_pool[1], 8)
        for h in range(2):
            cols = slice(h * half, (h + 1) * half)
            nc.vector.tensor_tensor(neg_s[:, cols], neg_kb[:, cols], scores[h][:], SUB)
        neg_m = keep.tile([P, 1], F32, name="neg_m")
        nc.vector.tensor_reduce(neg_m[:], neg_s[:], AXIS_X, MIN)

        p = keep.tile([P, PACK, P], F32, name="p")
        total = keep.tile([P, 1], F32, name="total")
        nc.scalar.activation(
            p[:].rearrange("q t s -> q s t"),
            neg_s[:].rearrange("q (s t) -> q s t", t=PACK),
            ACT.Exp,
            bias=neg_m[:],
            scale=-1.0,
            accum_out=total[:],
        )
        p_turned = psum.tile([P, PACK, NQ], F32, name="p_turned", tag="bank_p")
        for t in range(PACK):
            nc.tensor.transpose(p_turned[:, t, :], p[:, t, :], ident[:])
        turn_values(0)
        gather_values(1)
        quantize_values(0)
        w = keep.tile([P, NQ, PACK], BF16, name="w", align_bytes=64)
        w_codes = keep.tile([P, NQ], U32, name="w_codes", align_bytes=64)
        w_scales = keep.tile([P, NQ], U8, name="w_scales", align_bytes=64)
        nc.vector.tensor_tensor(
            w[:],
            p_turned[:].rearrange("s t q -> s q t"),
            vs_cols[:].unsqueeze(1).to_broadcast([P, NQ, PACK]),
            MULT,
        )
        turn_values(1)
        nc.vector.quantize_mx(
            out=w_codes[:].bitcast(FP8X4), scales=w_scales[:], in_=w[:].rearrange("p q t -> p (q t)")
        )
        quantize_values(1)
        inv_total = keep.tile([P, 1], F32, name="inv_total")
        nc.vector.reciprocal(inv_total[:], total[:])

        gate_tanh = keep.tile([P, DV], F32, name="gate_tanh")
        gate = keep.tile([P, DV], F32, name="gate")
        nc.scalar.activation(gate_tanh[:], gate_raw[:], ACT.Tanh, scale=0.5)
        nc.vector.tensor_scalar(gate[:], gate_tanh[:], 1.0, inv_total[:], ADD, MULT)

        result = keep.tile([P, DV], F32, name="result")
        out_rows = out.rearrange("b q e -> (b q) e")
        y = []
        for b in range(2):
            cols = slice(b * P, (b + 1) * P)
            acc = psum.tile([P, P], F32, name="y%d" % b, tag="bank_%s" % "ab"[b])
            nc.tensor.matmul_mx(
                out=acc[:],
                lhsT=w_codes[:].bitcast(FP8X4),
                lhsT_scale=w_scales[:],
                rhs=v_codes[:, cols].bitcast(FP8X4),
                rhs_scale=v_scales[:, cols],
                start=True,
                stop=True,
            )
            y.append(acc)
        for b in range(2):
            cols = slice(b * P, (b + 1) * P)
            nc.vector.scalar_tensor_tensor(result[:, cols], y[b][:], 0.5, gate[:, cols], MULT, MULT)
            nc.sync.dma_start(out=out_rows[:, cols], in_=result[:, cols])
